import numpy as np
import ml_dtypes


def mxq(x, axis, fmt="e4m3"):
    dtype, down = {"e4m3": (ml_dtypes.float8_e4m3fn, 7), "e5m2": (ml_dtypes.float8_e5m2, 14)}[fmt]
    v = np.moveaxis(np.asarray(x, np.float32).astype(ml_dtypes.bfloat16).astype(np.float64), axis, -1)
    blocks = v.reshape(v.shape[:-1] + (-1, 32))
    amax = np.abs(blocks).max(-1, keepdims=True)
    byte = np.maximum(np.where(amax > 0, np.frexp(amax)[1] - 1 + 127, 0) - down, 1)
    scale = np.exp2(byte - 127.0)
    codes = (blocks / scale).astype(np.float32).astype(dtype).astype(np.float64)
    return np.moveaxis((codes * scale).reshape(v.shape), -1, axis)


WIDE = False


def mx_kscale(k):
    if not WIDE:
        return np.ones(k)
    levels = np.array([10, -10, 5, -5, 0])
    if k % 512:
        return np.exp2(np.random.permutation(np.resize(levels, k // 32))).repeat(32)
    a = np.empty((k // 512, 16))
    for p in range(k // 512):
        a[p, :8] = np.random.permutation(np.resize(levels, 8))
        for g in range(8):
            far = levels[np.abs(levels - a[p, g]) >= 10]
            a[p, g + 8] = far[np.random.randint(len(far))]
    return np.exp2(a.ravel()).repeat(32)


def f64(x):
    return np.asarray(x).astype(np.float64)


def striped(idx):
    return np.tile(idx.reshape(-1, 16).T, (8, 1)).astype(np.uint16)


def unstriped(offs):
    return offs[:16].T.reshape(-1).astype(np.int64)


def striped8(idx):
    return np.concatenate([x.reshape(-1, 16).T for x in idx]).astype(np.uint16)


def runs(offs, k):
    lists = np.stack([offs[16 * r : 16 * r + 16].T.reshape(-1) for r in range(8)]).astype(np.int64)
    return lists[np.arange(k) % 512 // 64]


def pack_weight(w):
    k, n = w.shape
    w = f64(np.asarray(w, np.float32).astype(ml_dtypes.bfloat16)).reshape(k // 32, 32, n)
    amax = np.abs(w).max(1)
    byte = np.clip(np.where(amax > 0, np.frexp(amax)[1] - 1 + 127 - 7, 1), 1, 254)
    scaled = (w * np.exp2(127.0 - byte)[:, None, :]).reshape(k, n).astype(np.float32)
    words = np.ascontiguousarray(scaled.reshape(k // 512, 128, 4, n).transpose(0, 1, 3, 2)).astype(ml_dtypes.float8_e4m3fn).view(np.uint8)
    return words, np.ascontiguousarray(byte.astype(np.uint8).reshape(k // 512, 16, n))


def unpack_weight(words, scales):
    g, p, n, _ = words.shape
    vals = np.ascontiguousarray(words).view(ml_dtypes.float8_e4m3fn).astype(np.float64) * np.repeat(np.exp2(scales.astype(np.float64) - 127.0), 8, axis=1)[..., None]
    return vals.transpose(0, 1, 3, 2).reshape(g * 512, n)


K, T, S, G, H, C, W = 512, 1024, 512, 2048, 512, 512, 256


def setup_inputs():
    n = np.random.standard_normal
    s = mx_kscale(K)[:, None]
    packed_xT = pack_weight(n((K, T)) * s)
    packed_dT = pack_weight(n((K, G)) / s)
    perm = np.stack([np.random.permutation(S) for _ in range(8)])
    return {
        "x_words": packed_xT[0],
        "x_scales": packed_xT[1],
        "d_words": packed_dT[0],
        "d_scales": packed_dT[1],
        "gs": (np.random.uniform(0.5, 1.5, (K, 1)) / s).astype(np.float32),
        "offs": striped(np.random.permutation(T)[:S]),
        "k1": striped8(np.random.randint(0, G, (8, H))),
        "n1": striped8(np.stack([np.random.permutation(S) for _ in range(8)])),
        "n2": striped8(np.stack([np.random.permutation(S) for _ in range(8)])),
        "cand": striped(np.random.permutation(T)[:C]),
        "n3": striped8(perm[:, :W]),
        "n4": striped8(perm[:, W:]),
    }


def reference(x_words, x_scales, d_words, d_scales, gs, offs, k1, n1, n2, cand, n3, n4):
    x_cand = unpack_weight(x_words, x_scales)[:, unstriped(cand)]
    d_k1 = unpack_weight(d_words, d_scales)[np.arange(K)[:, None], runs(k1, K)]
    xq = unpack_weight(x_words, x_scales)[:, unstriped(offs)]
    h = 0.0625 * (d_k1.T @ xq)
    st = h + h[np.arange(H)[:, None], runs(n1, H)]
    z = f64(gs) * (st * (np.tanh(st[np.arange(H)[:, None], runs(n2, H)])))
    s = 0.0625 * ((x_cand.T @ mxq(z, 0, "e4m3")))
    pa = s[np.arange(C)[:, None], runs(n3, C)]
    pb = s[np.arange(C)[:, None], runs(n4, C)]
    ra = np.maximum(pa, pb)
    out = s.copy()
    out[np.arange(C)[:, None], runs(n3, C)] = ra
    return out

@@ -1,0 +1,204 @@
+from contextlib import ExitStack
+
+import concourse.mybir as mybir
+
+K, T, S, G, H, C, W = 512, 1024, 512, 2048, 512, 512, 256
+FLOPS = 2 * K * H * S + 2 * K * C * S
+
+F32 = mybir.dt.float32
+BF16 = mybir.dt.bfloat16
+I32 = mybir.dt.int32
+U32 = mybir.dt.uint32
+U16 = mybir.dt.uint16
+U8 = mybir.dt.uint8
+FP8X4 = mybir.dt.float8_e4m3fn_x4
+ALU = mybir.AluOpType
+ACT = mybir.ActivationFunctionType
+
+P = 128
+PACK = 4
+SIXTEENTH = 0.0625
+HALF = S // 2
+CHUNKS = ((0, 256), (256, 384), (384, 512))
+
+
+def tile_picked_pqchoppfill_none_p_kernel(tc, x_words, x_scales, d_words, d_scales, gs, offs, k1, n1, n2, cand, n3, n4, out):
+    nc = tc.nc
+    with ExitStack() as ctx:
+        lists = ctx.enter_context(tc.tile_pool(name="lists", bufs=1))
+        sb = ctx.enter_context(tc.tile_pool(name="sb", bufs=1))
+        psum = ctx.enter_context(tc.psum_pool(name="psum", bufs=1))
+
+        def load_list(src, name):
+            tile = lists.tile(list(src.shape), U16, name=name)
+            nc.sync.dma_start(tile[:], src)
+            return tile
+
+        def new(shape, dtype, name, tag=None):
+            return sb.tile(shape, dtype, name=name, tag=tag or name, align_bytes=64)
+
+        k1_sb = load_list(k1, "k1_sb")
+        d_bytes = new([P, G], U8, "d_bytes")
+        nc.sync.dma_start(d_bytes[:].bitcast(I32), d_scales[0].bitcast(I32).unsqueeze(1).to_broadcast([16, 8, G // 4]))
+        offs_sb = load_list(offs, "offs_sb")
+        x_table = new([P, T], I32, "x_table")
+        nc.sync.dma_start(x_table[:], x_words[0].rearrange("p n t -> p (n t)").bitcast(I32))
+        d_table = new([P, G], I32, "d_table")
+        nc.sync.dma_start(d_table[:], d_words[0].rearrange("p n t -> p (n t)").bitcast(I32))
+        x_bytes = new([P, T], U8, "x_bytes")
+        for q in range(4):
+            rows = x_scales[0, 4 * q : 4 * q + 4, :].bitcast(I32)
+            nc.scalar.dma_start(x_bytes[32 * q : 32 * q + 32, :].bitcast(I32), rows.unsqueeze(0).to_broadcast([8, 4, T // 4]))
+        gs_sb = new([P, PACK], F32, "gs_sb")
+        nc.sync.dma_start(gs_sb[:], gs.rearrange("(p t) o -> p (t o)", t=PACK))
+        cand_sb = load_list(cand, "cand_sb")
+        n1_sb = load_list(n1, "n1_sb")
+        n2_sb = load_list(n2, "n2_sb")
+        n3_sb = load_list(n3, "n3_sb")
+        n4_sb = load_list(n4, "n4_sb")
+
+        gs_h = new([P, PACK], F32, "gs_h")
+        nc.scalar.activation(gs_h[:], gs_sb[:], ACT.Copy, scale=SIXTEENTH)
+
+        d_plane = new([P, H], U8, "d_plane")
+        nc.gpsimd.memset(d_plane[:], 0)
+
+        d_bytes_picked = new([P, H], U8, "d_bytes_picked")
+        nc.vector.tensor_copy(d_bytes_picked[:], d_bytes[:].indirect(k1_sb[:]))
+        d_bytes_dealt = new([P, H], U8, "d_bytes_dealt")
+        nc.vector.tensor_copy(
+            d_bytes_dealt[:].rearrange("p (t m) -> p m t", t=PACK), d_bytes_picked[:].rearrange("p (m t) -> p m t", t=PACK)
+        )
+        for q in range(4):
+            nc.scalar.dma_start(
+                d_plane[32 * q : 32 * q + 4, :].bitcast(I32), d_bytes_dealt[32 * q : 32 * q + 32 : 8, :].bitcast(I32)
+            )
+        xq_codes = new([P, S], U32, "xq_codes")
+        nc.vector.tensor_copy(xq_codes[:], x_table[:].bitcast(U32).indirect(offs_sb[:]))
+        xq_plane = new([P, S], U8, "xq_plane")
+        nc.vector.tensor_copy(xq_plane[:], x_bytes[:].indirect(offs_sb[:]))
+        d_picked = [new([P, H // 2], U32, "d_picked%d" % u, "late%d" % u) for u in range(2)]
+        for u in range(2):
+            nc.vector.tensor_copy(d_picked[u][:], d_table[:].bitcast(U32).indirect(k1_sb[:, 16 * u : 16 * u + 16]))
+        d_codes = new([P, H], U32, "d_codes")
+        for u in range(2):
+            nc.vector.tensor_copy(
+                d_codes[:].rearrange("p (t m) -> p m t", t=PACK)[:, 64 * u : 64 * u + 64, :],
+                d_picked[u][:].rearrange("p (m t) -> p m t", t=PACK),
+            )
+
+        h_ps = [psum.tile([P, S], F32, name="h_ps%d" % t) for t in range(PACK)]
+        for t in range(PACK):
+            cols = slice(P * t, P * (t + 1))
+            nc.tensor.matmul_mx(
+                h_ps[t][:],
+                lhsT=d_codes[:, cols].bitcast(FP8X4),
+                lhsT_scale=d_plane[:, cols],
+                rhs=xq_codes[:].bitcast(FP8X4),
+                rhs_scale=xq_plane[:],
+                start=True,
+                stop=True,
+            )
+
+        gs_safe = new([P, PACK], F32, "gs_safe")
+        nc.vector.scalar_tensor_tensor(gs_safe[:], gs_sb[:], 0.0, gs_sb[:], ALU.is_equal, ALU.add)
+        gs_inv = new([P, PACK], F32, "gs_inv")
+        nc.vector.reciprocal(gs_inv[:], gs_safe[:])
+
+        cand_codes = new([P, C], U32, "cand_codes", "late0")
+        nc.vector.tensor_copy(
+            cand_codes[:].rearrange("p (t b v) -> p b t v", t=PACK, v=8), x_table[:].bitcast(U32).indirect(cand_sb[:])
+        )
+        cand_bytes = new([P, C], U8, "cand_bytes", "late1")
+        nc.vector.tensor_copy(cand_bytes[:], x_bytes[:].indirect(cand_sb[:]))
+        cand_plane = new([P, C], U8, "cand_plane")
+        nc.vector.tensor_copy(
+            cand_plane[:].bitcast(I32).rearrange("p (t b v) -> p b t v", t=PACK, v=2),
+            cand_bytes[:].bitcast(I32).rearrange("p (b t v) -> p b t v", t=PACK, v=2),
+        )
+
+        st = [new([P, S], F32, "st%d" % t) for t in range(PACK)]
+        th = [new([P, S], F32, "th%d" % t) for t in range(PACK)]
+        z32 = [new([P, PACK, b - a], F32, "z32_%d" % a) for a, b in CHUNKS]
+        s_ps = [psum.tile([P, S], F32, name="s_ps%d" % t) for t in range(PACK)]
+        s_sb = [new([P, S], F32, "s_sb%d" % t) for t in range(PACK)]
+
+        def make_st(t):
+            window = new([P, S], F32, "h_window%d" % t)
+            plain = new([P, S], F32, "h_plain%d" % t)
+            nc.scalar.activation(window[:], h_ps[t][:], ACT.Copy, scale=gs_h[:, t : t + 1])
+            nc.scalar.activation(plain[:], h_ps[t][:], ACT.Copy, scale=gs_h[:, t : t + 1])
+            for a in range(0, S, HALF):
+                picked = window[:].indirect(n1_sb[:, a // 16 : (a + HALF) // 16])
+                nc.vector.tensor_tensor(st[t][:, a : a + HALF], picked, plain[:, a : a + HALF], ALU.add)
+
+        def make_tanh(t):
+            nc.scalar.activation(th[t][:], st[t][:], ACT.Tanh, scale=gs_inv[:, t : t + 1])
+
+        def make_z(t, c):
+            a, b = CHUNKS[c]
+            nc.vector.tensor_tensor(z32[c][:, t, :], th[t][:].indirect(n2_sb[:, a // 16 : b // 16]), st[t][:, a:b], ALU.mult)
+
+        z16 = [new([P, (b - a) * PACK], BF16, "z16_%d" % a) for a, b in CHUNKS]
+
+        def weave(c):
+            dst = z16[c][:].rearrange("p (c i t) -> p c t i", i=4, t=PACK)
+            src = z32[c][:].rearrange("p t (c i) -> p c t i", i=4)
+            if c == len(CHUNKS) - 1:
+                nc.vector.tensor_copy(dst, src)
+            else:
+                nc.scalar.copy(dst, src)
+
+        def score(c):
+            a, b = CHUNKS[c]
+            codes = new([P, b - a], U32, "z_codes%d" % c)
+            plane = new([P, b - a], U8, "z_plane%d" % c)
+            nc.vector.quantize_mx(codes[:].bitcast(FP8X4), plane[:], z16[c][:])
+            for t in range(PACK):
+                cols = slice(P * t, P * (t + 1))
+                nc.tensor.matmul_mx(
+                    s_ps[t][:, a:b],
+                    lhsT=cand_codes[:, cols].bitcast(FP8X4),
+                    lhsT_scale=cand_plane[:, cols],
+                    rhs=codes[:].bitcast(FP8X4),
+                    rhs_scale=plane[:],
+                    start=True,
+                    stop=True,
+                )
+                nc.scalar.activation(s_sb[t][:, a:b], s_ps[t][:, a:b], ACT.Copy, scale=SIXTEENTH)
+
+        make_st(0)
+        make_st(1)
+        for t in range(PACK):
+            make_tanh(t)
+            if t > 0:
+                make_z(t - 1, 0)
+            if t + 2 < PACK:
+                make_st(t + 2)
+        make_z(PACK - 1, 0)
+        for c in range(1, len(CHUNKS)):
+            weave(c - 1)
+            for t in range(PACK):
+                make_z(t, c)
+            score(c - 1)
+        weave(len(CHUNKS) - 1)
+        score(len(CHUNKS) - 1)
+
+        out_rows = out.rearrange("(b t v) c -> t b v c", t=PACK, v=8)
+        pa = [new([P, W], F32, "pa%d" % t) for t in range(PACK)]
+        pb = [new([P, W], F32, "pb%d" % t) for t in range(PACK)]
+        ra = [new([P, W], F32, "ra%d" % t) for t in range(PACK)]
+
+        def fetch(dst, t, which):
+            nc.vector.tensor_copy(dst[t][:], s_sb[t][:].indirect(which[:]))
+
+        fetch(pa, 0, n3_sb)
+        fetch(pb, 0, n4_sb)
+        for t in range(PACK):
+            if t + 1 < PACK:
+                fetch(pa, t + 1, n3_sb)
+            nc.vector.tensor_tensor(ra[t][:], pa[t][:], pb[t][:], ALU.max)
+            if t + 1 < PACK:
+                fetch(pb, t + 1, n4_sb)
+            nc.vector.tensor_copy(s_sb[t][:].indirect(n3_sb[:]), ra[t][:])
+            nc.sync.dma_start(out_rows[t], s_sb[t][:])

@@ -41,14 +41,14 @@ def tile_picked_pqchoppfill_none_p_kernel(tc, x_words, x_scales, d_words, d_scal
         d_bytes = new([P, G], U8, "d_bytes")
         nc.sync.dma_start(d_bytes[:].bitcast(I32), d_scales[0].bitcast(I32).unsqueeze(1).to_broadcast([16, 8, G // 4]))
         offs_sb = load_list(offs, "offs_sb")
-        x_table = new([P, T], I32, "x_table")
-        nc.sync.dma_start(x_table[:], x_words[0].rearrange("p n t -> p (n t)").bitcast(I32))
-        d_table = new([P, G], I32, "d_table")
-        nc.sync.dma_start(d_table[:], d_words[0].rearrange("p n t -> p (n t)").bitcast(I32))
         x_bytes = new([P, T], U8, "x_bytes")
         for q in range(4):
             rows = x_scales[0, 4 * q : 4 * q + 4, :].bitcast(I32)
             nc.scalar.dma_start(x_bytes[32 * q : 32 * q + 32, :].bitcast(I32), rows.unsqueeze(0).to_broadcast([8, 4, T // 4]))
+        d_table = new([P, G], I32, "d_table")
+        nc.sync.dma_start(d_table[:], d_words[0].rearrange("p n t -> p (n t)").bitcast(I32))
+        x_table = new([P, T], I32, "x_table")
+        nc.sync.dma_start(x_table[:], x_words[0].rearrange("p n t -> p (n t)").bitcast(I32))
         gs_sb = new([P, PACK], F32, "gs_sb")
         nc.sync.dma_start(gs_sb[:], gs.rearrange("(p t) o -> p (t o)", t=PACK))
         cand_sb = load_list(cand, "cand_sb")
@@ -73,8 +73,6 @@ def tile_picked_pqchoppfill_none_p_kernel(tc, x_words, x_scales, d_words, d_scal
             nc.scalar.dma_start(
                 d_plane[32 * q : 32 * q + 4, :].bitcast(I32), d_bytes_dealt[32 * q : 32 * q + 32 : 8, :].bitcast(I32)
             )
-        xq_codes = new([P, S], U32, "xq_codes")
-        nc.vector.tensor_copy(xq_codes[:], x_table[:].bitcast(U32).indirect(offs_sb[:]))
         xq_plane = new([P, S], U8, "xq_plane")
         nc.vector.tensor_copy(xq_plane[:], x_bytes[:].indirect(offs_sb[:]))
         d_picked = [new([P, H // 2], U32, "d_picked%d" % u, "late%d" % u) for u in range(2)]
@@ -87,15 +85,22 @@ def tile_picked_pqchoppfill_none_p_kernel(tc, x_words, x_scales, d_words, d_scal
                 d_picked[u][:].rearrange("p (m t) -> p m t", t=PACK),
             )
 
-        h_ps = [psum.tile([P, S], F32, name="h_ps%d" % t) for t in range(PACK)]
-        for t in range(PACK):
+        xq_codes = new([P, S], U32, "xq_codes")
+        for u in range(2):
+            picked = x_table[:].bitcast(U32).indirect(offs_sb[:, 16 * u : 16 * u + 16])
+            nc.vector.tensor_copy(xq_codes[:, u * HALF : (u + 1) * HALF], picked)
+
+        h_parts = [(0, 0, HALF, "bank7"), (0, HALF, S, "bank0")] + [(t, 0, S, "bank%d" % t) for t in range(1, PACK)]
+        h_ps = {}
+        for t, a, b, bank in h_parts:
             cols = slice(P * t, P * (t + 1))
+            h_ps[t, a] = psum.tile([P, b - a], F32, name="h_ps%d_%d" % (t, a), tag=bank)
             nc.tensor.matmul_mx(
-                h_ps[t][:],
+                h_ps[t, a][:],
                 lhsT=d_codes[:, cols].bitcast(FP8X4),
                 lhsT_scale=d_plane[:, cols],
-                rhs=xq_codes[:].bitcast(FP8X4),
-                rhs_scale=xq_plane[:],
+                rhs=xq_codes[:, a:b].bitcast(FP8X4),
+                rhs_scale=xq_plane[:, a:b],
                 start=True,
                 stop=True,
             )
@@ -117,31 +122,42 @@ def tile_picked_pqchoppfill_none_p_kernel(tc, x_words, x_scales, d_words, d_scal
             cand_bytes[:].bitcast(I32).rearrange("p (b t v) -> p b t v", t=PACK, v=2),
         )
 
-        st = [new([P, S], F32, "st%d" % t) for t in range(PACK)]
+        st = [[new([P, HALF], F32, "st%d_%d" % (t, u)) for u in range(2)] for t in range(PACK)]
         th = [new([P, S], F32, "th%d" % t) for t in range(PACK)]
-        z32 = [new([P, PACK, b - a], F32, "z32_%d" % a) for a, b in CHUNKS]
-        s_ps = [psum.tile([P, S], F32, name="s_ps%d" % t) for t in range(PACK)]
+        z32_tags = ("z32_0", "st3_0", "z16_0")
+        z16_tags = ("z16_0", "z16_1", "z16_1")
+        z32 = {}
+        z16 = {}
+        s_ps = {}
         s_sb = [new([P, S], F32, "s_sb%d" % t) for t in range(PACK)]
 
         def make_st(t):
             window = new([P, S], F32, "h_window%d" % t)
             plain = new([P, S], F32, "h_plain%d" % t)
-            nc.scalar.activation(window[:], h_ps[t][:], ACT.Copy, scale=gs_h[:, t : t + 1])
-            nc.scalar.activation(plain[:], h_ps[t][:], ACT.Copy, scale=gs_h[:, t : t + 1])
-            for a in range(0, S, HALF):
+            for part, a, b, bank in h_parts:
+                if part == t:
+                    nc.scalar.activation(window[:, a:b], h_ps[t, a][:], ACT.Copy, scale=gs_h[:, t : t + 1])
+                    nc.scalar.activation(plain[:, a:b], h_ps[t, a][:], ACT.Copy, scale=gs_h[:, t : t + 1])
+            for u in range(2):
+                a = u * HALF
                 picked = window[:].indirect(n1_sb[:, a // 16 : (a + HALF) // 16])
-                nc.vector.tensor_tensor(st[t][:, a : a + HALF], picked, plain[:, a : a + HALF], ALU.add)
+                nc.vector.tensor_tensor(st[t][u][:], picked, plain[:, a : a + HALF], ALU.add)
 
         def make_tanh(t):
-            nc.scalar.activation(th[t][:], st[t][:], ACT.Tanh, scale=gs_inv[:, t : t + 1])
+            for u in range(2):
+                nc.scalar.activation(th[t][:, u * HALF : (u + 1) * HALF], st[t][u][:], ACT.Tanh, scale=gs_inv[:, t : t + 1])
 
         def make_z(t, c):
             a, b = CHUNKS[c]
-            nc.vector.tensor_tensor(z32[c][:, t, :], th[t][:].indirect(n2_sb[:, a // 16 : b // 16]), st[t][:, a:b], ALU.mult)
-
-        z16 = [new([P, (b - a) * PACK], BF16, "z16_%d" % a) for a, b in CHUNKS]
+            if t == 0:
+                z32[c] = new([P, PACK, b - a], F32, "z32_%d" % c, z32_tags[c])
+            u, a0 = divmod(a, HALF)
+            picked = th[t][:].indirect(n2_sb[:, a // 16 : b // 16])
+            nc.vector.tensor_tensor(z32[c][:, t, :], picked, st[t][u][:, a0 : a0 + b - a], ALU.mult)
 
         def weave(c):
+            a, b = CHUNKS[c]
+            z16[c] = new([P, (b - a) * PACK], BF16, "z16_%d" % c, z16_tags[c])
             dst = z16[c][:].rearrange("p (c i t) -> p c t i", i=4, t=PACK)
             src = z32[c][:].rearrange("p t (c i) -> p c t i", i=4)
             if c == len(CHUNKS) - 1:
@@ -156,6 +172,8 @@ def tile_picked_pqchoppfill_none_p_kernel(tc, x_words, x_scales, d_words, d_scal
             nc.vector.quantize_mx(codes[:].bitcast(FP8X4), plane[:], z16[c][:])
             for t in range(PACK):
                 cols = slice(P * t, P * (t + 1))
+                if c == 0:
+                    s_ps[t] = psum.tile([P, S], F32, name="s_ps%d" % t, tag="bank%d" % (PACK + t))
                 nc.tensor.matmul_mx(
                     s_ps[t][:, a:b],
                     lhsT=cand_codes[:, cols].bitcast(FP8X4),
@@ -176,29 +194,24 @@ def tile_picked_pqchoppfill_none_p_kernel(tc, x_words, x_scales, d_words, d_scal
             if t + 2 < PACK:
                 make_st(t + 2)
         make_z(PACK - 1, 0)
+        weave(0)
         for c in range(1, len(CHUNKS)):
-            weave(c - 1)
             for t in range(PACK):
                 make_z(t, c)
             score(c - 1)
-        weave(len(CHUNKS) - 1)
+            weave(c)
         score(len(CHUNKS) - 1)
 
         out_rows = out.rearrange("(b t v) c -> t b v c", t=PACK, v=8)
         pa = [new([P, W], F32, "pa%d" % t) for t in range(PACK)]
-        pb = [new([P, W], F32, "pb%d" % t) for t in range(PACK)]
-        ra = [new([P, W], F32, "ra%d" % t) for t in range(PACK)]
-
-        def fetch(dst, t, which):
-            nc.vector.tensor_copy(dst[t][:], s_sb[t][:].indirect(which[:]))
-
-        fetch(pa, 0, n3_sb)
-        fetch(pb, 0, n4_sb)
+        gap = [new([P, W], F32, "gap%d" % t) for t in range(PACK)]
+        rise = [new([P, W], F32, "rise%d" % t) for t in range(PACK)]
+        for pair in range(0, PACK, 2):
+            for t in (pair, pair + 1):
+                nc.vector.tensor_copy(pa[t][:], s_sb[t][:].indirect(n3_sb[:]))
+            for t in (pair, pair + 1):
+                nc.vector.tensor_tensor(gap[t][:], s_sb[t][:].indirect(n4_sb[:]), pa[t][:], ALU.subtract)
+                nc.scalar.activation(rise[t][:], gap[t][:], ACT.Relu)
         for t in range(PACK):
-            if t + 1 < PACK:
-                fetch(pa, t + 1, n3_sb)
-            nc.vector.tensor_tensor(ra[t][:], pa[t][:], pb[t][:], ALU.max)
-            if t + 1 < PACK:
-                fetch(pb, t + 1, n4_sb)
-            nc.vector.tensor_copy(s_sb[t][:].indirect(n3_sb[:]), ra[t][:])
+            nc.vector.tensor_tensor(s_sb[t][:].indirect(n3_sb[:]), pa[t][:], rise[t][:], ALU.add)
             nc.sync.dma_start(out_rows[t], s_sb[t][:])

@@ -41,14 +41,14 @@ def tile_picked_pqchoppfill_none_p_kernel(tc, x_words, x_scales, d_words, d_scal
         d_bytes = new([P, G], U8, "d_bytes")
         nc.sync.dma_start(d_bytes[:].bitcast(I32), d_scales[0].bitcast(I32).unsqueeze(1).to_broadcast([16, 8, G // 4]))
         offs_sb = load_list(offs, "offs_sb")
+        x_table = new([P, T], I32, "x_table")
+        nc.sync.dma_start(x_table[:], x_words[0].rearrange("p n t -> p (n t)").bitcast(I32))
+        d_table = new([P, G], I32, "d_table")
+        nc.sync.dma_start(d_table[:], d_words[0].rearrange("p n t -> p (n t)").bitcast(I32))
         x_bytes = new([P, T], U8, "x_bytes")
         for q in range(4):
             rows = x_scales[0, 4 * q : 4 * q + 4, :].bitcast(I32)
             nc.scalar.dma_start(x_bytes[32 * q : 32 * q + 32, :].bitcast(I32), rows.unsqueeze(0).to_broadcast([8, 4, T // 4]))
-        d_table = new([P, G], I32, "d_table")
-        nc.sync.dma_start(d_table[:], d_words[0].rearrange("p n t -> p (n t)").bitcast(I32))
-        x_table = new([P, T], I32, "x_table")
-        nc.sync.dma_start(x_table[:], x_words[0].rearrange("p n t -> p (n t)").bitcast(I32))
         gs_sb = new([P, PACK], F32, "gs_sb")
         nc.sync.dma_start(gs_sb[:], gs.rearrange("(p t) o -> p (t o)", t=PACK))
         cand_sb = load_list(cand, "cand_sb")
@@ -65,6 +65,8 @@ def tile_picked_pqchoppfill_none_p_kernel(tc, x_words, x_scales, d_words, d_scal
 
         d_bytes_picked = new([P, H], U8, "d_bytes_picked")
         nc.vector.tensor_copy(d_bytes_picked[:], d_bytes[:].indirect(k1_sb[:]))
+        xq_plane = new([P, S], U8, "xq_plane")
+        nc.vector.tensor_copy(xq_plane[:], x_bytes[:].indirect(offs_sb[:]))
         d_bytes_dealt = new([P, H], U8, "d_bytes_dealt")
         nc.vector.tensor_copy(
             d_bytes_dealt[:].rearrange("p (t m) -> p m t", t=PACK), d_bytes_picked[:].rearrange("p (m t) -> p m t", t=PACK)
@@ -73,8 +75,8 @@ def tile_picked_pqchoppfill_none_p_kernel(tc, x_words, x_scales, d_words, d_scal
             nc.scalar.dma_start(
                 d_plane[32 * q : 32 * q + 4, :].bitcast(I32), d_bytes_dealt[32 * q : 32 * q + 32 : 8, :].bitcast(I32)
             )
-        xq_plane = new([P, S], U8, "xq_plane")
-        nc.vector.tensor_copy(xq_plane[:], x_bytes[:].indirect(offs_sb[:]))
+        xq_codes = new([P, S], U32, "xq_codes")
+        nc.vector.tensor_copy(xq_codes[:], x_table[:].bitcast(U32).indirect(offs_sb[:]))
         d_picked = [new([P, H // 2], U32, "d_picked%d" % u, "late%d" % u) for u in range(2)]
         for u in range(2):
             nc.vector.tensor_copy(d_picked[u][:], d_table[:].bitcast(U32).indirect(k1_sb[:, 16 * u : 16 * u + 16]))
@@ -85,37 +87,32 @@ def tile_picked_pqchoppfill_none_p_kernel(tc, x_words, x_scales, d_words, d_scal
                 d_picked[u][:].rearrange("p (m t) -> p m t", t=PACK),
             )
 
-        xq_codes = new([P, S], U32, "xq_codes")
-        for u in range(2):
-            picked = x_table[:].bitcast(U32).indirect(offs_sb[:, 16 * u : 16 * u + 16])
-            nc.vector.tensor_copy(xq_codes[:, u * HALF : (u + 1) * HALF], picked)
-
-        h_parts = [(0, 0, HALF, "bank7"), (0, HALF, S, "bank0")] + [(t, 0, S, "bank%d" % t) for t in range(1, PACK)]
-        h_ps = {}
-        for t, a, b, bank in h_parts:
+        h_ps = [psum.tile([P, S], F32, name="h_ps%d" % t) for t in range(PACK)]
+        for t in range(PACK):
             cols = slice(P * t, P * (t + 1))
-            h_ps[t, a] = psum.tile([P, b - a], F32, name="h_ps%d_%d" % (t, a), tag=bank)
             nc.tensor.matmul_mx(
-                h_ps[t, a][:],
+                h_ps[t][:],
                 lhsT=d_codes[:, cols].bitcast(FP8X4),
                 lhsT_scale=d_plane[:, cols],
-                rhs=xq_codes[:, a:b].bitcast(FP8X4),
-                rhs_scale=xq_plane[:, a:b],
+                rhs=xq_codes[:].bitcast(FP8X4),
+                rhs_scale=xq_plane[:],
                 start=True,
                 stop=True,
             )
 
+        gs_zero = new([P, PACK], F32, "gs_zero")
+        nc.gpsimd.tensor_scalar(gs_zero[:], gs_sb[:], 0.0, None, ALU.is_equal)
         gs_safe = new([P, PACK], F32, "gs_safe")
-        nc.vector.scalar_tensor_tensor(gs_safe[:], gs_sb[:], 0.0, gs_sb[:], ALU.is_equal, ALU.add)
+        nc.gpsimd.tensor_tensor(gs_safe[:], gs_sb[:], gs_zero[:], ALU.add)
         gs_inv = new([P, PACK], F32, "gs_inv")
         nc.vector.reciprocal(gs_inv[:], gs_safe[:])
 
-        cand_codes = new([P, C], U32, "cand_codes", "late0")
+        cand_bytes = new([P, C], U8, "cand_bytes", "late0")
+        nc.vector.tensor_copy(cand_bytes[:], x_bytes[:].indirect(cand_sb[:]))
+        cand_codes = new([P, C], U32, "cand_codes", "late1")
         nc.vector.tensor_copy(
             cand_codes[:].rearrange("p (t b v) -> p b t v", t=PACK, v=8), x_table[:].bitcast(U32).indirect(cand_sb[:])
         )
-        cand_bytes = new([P, C], U8, "cand_bytes", "late1")
-        nc.vector.tensor_copy(cand_bytes[:], x_bytes[:].indirect(cand_sb[:]))
         cand_plane = new([P, C], U8, "cand_plane")
         nc.vector.tensor_copy(
             cand_plane[:].bitcast(I32).rearrange("p (t b v) -> p b t v", t=PACK, v=2),
@@ -128,16 +125,14 @@ def tile_picked_pqchoppfill_none_p_kernel(tc, x_words, x_scales, d_words, d_scal
         z16_tags = ("z16_0", "z16_1", "z16_1")
         z32 = {}
         z16 = {}
-        s_ps = {}
+        s_ps = [psum.tile([P, S], F32, name="s_ps%d" % t) for t in range(PACK)]
         s_sb = [new([P, S], F32, "s_sb%d" % t) for t in range(PACK)]
 
         def make_st(t):
             window = new([P, S], F32, "h_window%d" % t)
             plain = new([P, S], F32, "h_plain%d" % t)
-            for part, a, b, bank in h_parts:
-                if part == t:
-                    nc.scalar.activation(window[:, a:b], h_ps[t, a][:], ACT.Copy, scale=gs_h[:, t : t + 1])
-                    nc.scalar.activation(plain[:, a:b], h_ps[t, a][:], ACT.Copy, scale=gs_h[:, t : t + 1])
+            nc.scalar.activation(window[:], h_ps[t][:], ACT.Copy, scale=gs_h[:, t : t + 1])
+            nc.scalar.activation(plain[:], h_ps[t][:], ACT.Copy, scale=gs_h[:, t : t + 1])
             for u in range(2):
                 a = u * HALF
                 picked = window[:].indirect(n1_sb[:, a // 16 : (a + HALF) // 16])
@@ -172,8 +167,6 @@ def tile_picked_pqchoppfill_none_p_kernel(tc, x_words, x_scales, d_words, d_scal
             nc.vector.quantize_mx(codes[:].bitcast(FP8X4), plane[:], z16[c][:])
             for t in range(PACK):
                 cols = slice(P * t, P * (t + 1))
-                if c == 0:
-                    s_ps[t] = psum.tile([P, S], F32, name="s_ps%d" % t, tag="bank%d" % (PACK + t))
                 nc.tensor.matmul_mx(
                     s_ps[t][:, a:b],
                     lhsT=cand_codes[:, cols].bitcast(FP8X4),

@@ -17,6 +17,10 @@ ACT = mybir.ActivationFunctionType
 
 P = 128
 PACK = 4
+QUADRANT = 32
+BLOCK = 8
+ENTRIES = 16
+LINE = 4
 SIXTEENTH = 0.0625
 HALF = S // 2
 CHUNKS = ((0, 256), (256, 384), (384, 512))
@@ -37,22 +41,30 @@ def tile_picked_pqchoppfill_none_p_kernel(tc, x_words, x_scales, d_words, d_scal
         def new(shape, dtype, name, tag=None):
             return sb.tile(shape, dtype, name=name, tag=tag or name, align_bytes=64)
 
+        def entries(list_tile, a, b):
+            return list_tile[:, a // ENTRIES : b // ENTRIES]
+
+        offs_sb = load_list(offs, "offs_sb")
+        x_bytes = new([P, T], U8, "x_bytes")
+        for q in range(P // QUADRANT):
+            rows = x_scales[0, PACK * q : PACK * (q + 1), :].bitcast(I32)
+            nc.sync.dma_start(
+                x_bytes[QUADRANT * q : QUADRANT * (q + 1), :].bitcast(I32),
+                rows.unsqueeze(0).to_broadcast([QUADRANT // PACK, PACK, T // PACK]),
+            )
         k1_sb = load_list(k1, "k1_sb")
         d_bytes = new([P, G], U8, "d_bytes")
-        nc.sync.dma_start(d_bytes[:].bitcast(I32), d_scales[0].bitcast(I32).unsqueeze(1).to_broadcast([16, 8, G // 4]))
-        offs_sb = load_list(offs, "offs_sb")
+        nc.sync.dma_start(
+            d_bytes[:].bitcast(I32), d_scales[0].bitcast(I32).unsqueeze(1).to_broadcast([P // BLOCK, BLOCK, G // PACK])
+        )
         x_table = new([P, T], I32, "x_table")
         nc.sync.dma_start(x_table[:], x_words[0].rearrange("p n t -> p (n t)").bitcast(I32))
-        d_table = new([P, G], I32, "d_table")
-        nc.sync.dma_start(d_table[:], d_words[0].rearrange("p n t -> p (n t)").bitcast(I32))
-        x_bytes = new([P, T], U8, "x_bytes")
-        for q in range(4):
-            rows = x_scales[0, 4 * q : 4 * q + 4, :].bitcast(I32)
-            nc.scalar.dma_start(x_bytes[32 * q : 32 * q + 32, :].bitcast(I32), rows.unsqueeze(0).to_broadcast([8, 4, T // 4]))
         gs_sb = new([P, PACK], F32, "gs_sb")
         nc.sync.dma_start(gs_sb[:], gs.rearrange("(p t) o -> p (t o)", t=PACK))
         cand_sb = load_list(cand, "cand_sb")
         n1_sb = load_list(n1, "n1_sb")
+        d_table = new([P, G], I32, "d_table")
+        nc.sync.dma_start(d_table[:], d_words[0].rearrange("p n t -> p (n t)").bitcast(I32))
         n2_sb = load_list(n2, "n2_sb")
         n3_sb = load_list(n3, "n3_sb")
         n4_sb = load_list(n4, "n4_sb")
@@ -63,28 +75,31 @@ def tile_picked_pqchoppfill_none_p_kernel(tc, x_words, x_scales, d_words, d_scal
         d_plane = new([P, H], U8, "d_plane")
         nc.gpsimd.memset(d_plane[:], 0)
 
-        d_bytes_picked = new([P, H], U8, "d_bytes_picked")
-        nc.vector.tensor_copy(d_bytes_picked[:], d_bytes[:].indirect(k1_sb[:]))
         xq_plane = new([P, S], U8, "xq_plane")
         nc.vector.tensor_copy(xq_plane[:], x_bytes[:].indirect(offs_sb[:]))
+        d_bytes_picked = new([P, H], U8, "d_bytes_picked")
+        nc.vector.tensor_copy(d_bytes_picked[:], d_bytes[:].indirect(k1_sb[:]))
         d_bytes_dealt = new([P, H], U8, "d_bytes_dealt")
         nc.vector.tensor_copy(
-            d_bytes_dealt[:].rearrange("p (t m) -> p m t", t=PACK), d_bytes_picked[:].rearrange("p (m t) -> p m t", t=PACK)
+            d_bytes_dealt[:].rearrange("p (t m) -> p t m", t=PACK), d_bytes_picked[:].rearrange("p (m t) -> p t m", t=PACK)
         )
-        for q in range(4):
+        for q in range(P // QUADRANT):
             nc.scalar.dma_start(
-                d_plane[32 * q : 32 * q + 4, :].bitcast(I32), d_bytes_dealt[32 * q : 32 * q + 32 : 8, :].bitcast(I32)
+                d_plane[QUADRANT * q : QUADRANT * q + PACK, :].bitcast(I32),
+                d_bytes_dealt[QUADRANT * q : QUADRANT * (q + 1) : BLOCK, :].bitcast(I32),
             )
         xq_codes = new([P, S], U32, "xq_codes")
         nc.vector.tensor_copy(xq_codes[:], x_table[:].bitcast(U32).indirect(offs_sb[:]))
-        d_picked = [new([P, H // 2], U32, "d_picked%d" % u, "late%d" % u) for u in range(2)]
+        d_picked = [new([P, H // 2], U32, "d_picked%d" % u) for u in range(2)]
         for u in range(2):
-            nc.vector.tensor_copy(d_picked[u][:], d_table[:].bitcast(U32).indirect(k1_sb[:, 16 * u : 16 * u + 16]))
+            picked = d_table[:].bitcast(U32).indirect(entries(k1_sb, u * H // 2, (u + 1) * H // 2))
+            nc.vector.tensor_copy(d_picked[u][:], picked)
         d_codes = new([P, H], U32, "d_codes")
+        lines = H // 2 // (PACK * LINE)
         for u in range(2):
             nc.vector.tensor_copy(
-                d_codes[:].rearrange("p (t m) -> p m t", t=PACK)[:, 64 * u : 64 * u + 64, :],
-                d_picked[u][:].rearrange("p (m t) -> p m t", t=PACK),
+                d_codes[:].rearrange("p (t c i) -> p c t i", t=PACK, i=LINE)[:, lines * u : lines * (u + 1), :, :],
+                d_picked[u][:].rearrange("p (c i t) -> p c t i", t=PACK, i=LINE),
             )
 
         h_ps = [psum.tile([P, S], F32, name="h_ps%d" % t) for t in range(PACK)]
@@ -104,25 +119,24 @@ def tile_picked_pqchoppfill_none_p_kernel(tc, x_words, x_scales, d_words, d_scal
         nc.gpsimd.tensor_scalar(gs_zero[:], gs_sb[:], 0.0, None, ALU.is_equal)
         gs_safe = new([P, PACK], F32, "gs_safe")
         nc.gpsimd.tensor_tensor(gs_safe[:], gs_sb[:], gs_zero[:], ALU.add)
-        gs_inv = new([P, PACK], F32, "gs_inv")
-        nc.vector.reciprocal(gs_inv[:], gs_safe[:])
 
-        cand_bytes = new([P, C], U8, "cand_bytes", "late0")
+        cand_bytes = new([P, C], U8, "cand_bytes", "d_table")
         nc.vector.tensor_copy(cand_bytes[:], x_bytes[:].indirect(cand_sb[:]))
-        cand_codes = new([P, C], U32, "cand_codes", "late1")
+        gs_inv = new([P, PACK], F32, "gs_inv", "d_picked1")
+        nc.vector.reciprocal(gs_inv[:], gs_safe[:])
+        cand_codes = new([P, C], U32, "cand_codes", "d_picked0")
         nc.vector.tensor_copy(
-            cand_codes[:].rearrange("p (t b v) -> p b t v", t=PACK, v=8), x_table[:].bitcast(U32).indirect(cand_sb[:])
+            cand_codes[:].rearrange("p (t b v) -> p b t v", t=PACK, v=BLOCK), x_table[:].bitcast(U32).indirect(cand_sb[:])
         )
         cand_plane = new([P, C], U8, "cand_plane")
         nc.vector.tensor_copy(
-            cand_plane[:].bitcast(I32).rearrange("p (t b v) -> p b t v", t=PACK, v=2),
-            cand_bytes[:].bitcast(I32).rearrange("p (b t v) -> p b t v", t=PACK, v=2),
+            cand_plane[:].bitcast(I32).rearrange("p (t b v) -> p b t v", t=PACK, v=BLOCK // PACK),
+            cand_bytes[:].bitcast(I32).rearrange("p (b t v) -> p b t v", t=PACK, v=BLOCK // PACK),
         )
 
         st = [[new([P, HALF], F32, "st%d_%d" % (t, u)) for u in range(2)] for t in range(PACK)]
         th = [new([P, S], F32, "th%d" % t) for t in range(PACK)]
-        z32_tags = ("z32_0", "st3_0", "z16_0")
-        z16_tags = ("z16_0", "z16_1", "z16_1")
+        z32_tags = ("z32_0", "d_picked1", "z32_0")
         z32 = {}
         z16 = {}
         s_ps = [psum.tile([P, S], F32, name="s_ps%d" % t) for t in range(PACK)]
@@ -134,9 +148,8 @@ def tile_picked_pqchoppfill_none_p_kernel(tc, x_words, x_scales, d_words, d_scal
             nc.scalar.activation(window[:], h_ps[t][:], ACT.Copy, scale=gs_h[:, t : t + 1])
             nc.scalar.activation(plain[:], h_ps[t][:], ACT.Copy, scale=gs_h[:, t : t + 1])
             for u in range(2):
-                a = u * HALF
-                picked = window[:].indirect(n1_sb[:, a // 16 : (a + HALF) // 16])
-                nc.vector.tensor_tensor(st[t][u][:], picked, plain[:, a : a + HALF], ALU.add)
+                a, b = u * HALF, (u + 1) * HALF
+                nc.vector.tensor_tensor(st[t][u][:], window[:].indirect(entries(n1_sb, a, b)), plain[:, a:b], ALU.add)
 
         def make_tanh(t):
             for u in range(2):
@@ -147,14 +160,14 @@ def tile_picked_pqchoppfill_none_p_kernel(tc, x_words, x_scales, d_words, d_scal
             if t == 0:
                 z32[c] = new([P, PACK, b - a], F32, "z32_%d" % c, z32_tags[c])
             u, a0 = divmod(a, HALF)
-            picked = th[t][:].indirect(n2_sb[:, a // 16 : b // 16])
+            picked = th[t][:].indirect(entries(n2_sb, a, b))
             nc.vector.tensor_tensor(z32[c][:, t, :], picked, st[t][u][:, a0 : a0 + b - a], ALU.mult)
 
-        def weave(c):
+        def round_z(c):
             a, b = CHUNKS[c]
-            z16[c] = new([P, (b - a) * PACK], BF16, "z16_%d" % c, z16_tags[c])
-            dst = z16[c][:].rearrange("p (c i t) -> p c t i", i=4, t=PACK)
-            src = z32[c][:].rearrange("p t (c i) -> p c t i", i=4)
+            z16[c] = new([P, (b - a) * PACK], BF16, "z16_%d" % c)
+            dst = z16[c][:].rearrange("p (n i t) -> p n t i", i=LINE, t=PACK)
+            src = z32[c][:].rearrange("p t (n i) -> p n t i", i=LINE)
             if c == len(CHUNKS) - 1:
                 nc.vector.tensor_copy(dst, src)
             else:
@@ -187,22 +200,22 @@ def tile_picked_pqchoppfill_none_p_kernel(tc, x_words, x_scales, d_words, d_scal
             if t + 2 < PACK:
                 make_st(t + 2)
         make_z(PACK - 1, 0)
-        weave(0)
+        round_z(0)
         for c in range(1, len(CHUNKS)):
             for t in range(PACK):
                 make_z(t, c)
             score(c - 1)
-            weave(c)
+            round_z(c)
         score(len(CHUNKS) - 1)
 
-        out_rows = out.rearrange("(b t v) c -> t b v c", t=PACK, v=8)
+        out_rows = out.rearrange("(b t v) c -> t b v c", t=PACK, v=BLOCK)
         pa = [new([P, W], F32, "pa%d" % t) for t in range(PACK)]
         gap = [new([P, W], F32, "gap%d" % t) for t in range(PACK)]
         rise = [new([P, W], F32, "rise%d" % t) for t in range(PACK)]
-        for pair in range(0, PACK, 2):
-            for t in (pair, pair + 1):
+        for first in range(0, PACK, 2):
+            for t in (first, first + 1):
                 nc.vector.tensor_copy(pa[t][:], s_sb[t][:].indirect(n3_sb[:]))
-            for t in (pair, pair + 1):
+            for t in (first, first + 1):
                 nc.vector.tensor_tensor(gap[t][:], s_sb[t][:].indirect(n4_sb[:]), pa[t][:], ALU.subtract)
                 nc.scalar.activation(rise[t][:], gap[t][:], ACT.Relu)
         for t in range(PACK):

from contextlib import ExitStack

import concourse.mybir as mybir

K, T, S, G, H, C, W = 512, 1024, 512, 2048, 512, 512, 256
FLOPS = 2 * K * H * S + 2 * K * C * S

F32 = mybir.dt.float32
BF16 = mybir.dt.bfloat16
I32 = mybir.dt.int32
U32 = mybir.dt.uint32
U16 = mybir.dt.uint16
U8 = mybir.dt.uint8
FP8X4 = mybir.dt.float8_e4m3fn_x4
ALU = mybir.AluOpType
ACT = mybir.ActivationFunctionType

P = 128
PACK = 4
QUADRANT = 32
BLOCK = 8
ENTRIES = 16
LINE = 4
SIXTEENTH = 0.0625
HALF = S // 2
CHUNKS = ((0, 256), (256, 384), (384, 512))


def tile_picked_pqchoppfill_none_p_kernel(tc, x_words, x_scales, d_words, d_scales, gs, offs, k1, n1, n2, cand, n3, n4, out):
    nc = tc.nc
    with ExitStack() as ctx:
        lists = ctx.enter_context(tc.tile_pool(name="lists", bufs=1))
        sb = ctx.enter_context(tc.tile_pool(name="sb", bufs=1))
        psum = ctx.enter_context(tc.psum_pool(name="psum", bufs=1))

        def load_list(src, name):
            tile = lists.tile(list(src.shape), U16, name=name)
            nc.sync.dma_start(tile[:], src)
            return tile

        def new(shape, dtype, name, tag=None):
            return sb.tile(shape, dtype, name=name, tag=tag or name, align_bytes=64)

        def entries(list_tile, a, b):
            return list_tile[:, a // ENTRIES : b // ENTRIES]

        offs_sb = load_list(offs, "offs_sb")
        x_bytes = new([P, T], U8, "x_bytes")
        for q in range(P // QUADRANT):
            rows = x_scales[0, PACK * q : PACK * (q + 1), :].bitcast(I32)
            nc.sync.dma_start(
                x_bytes[QUADRANT * q : QUADRANT * (q + 1), :].bitcast(I32),
                rows.unsqueeze(0).to_broadcast([QUADRANT // PACK, PACK, T // PACK]),
            )
        k1_sb = load_list(k1, "k1_sb")
        d_bytes = new([P, G], U8, "d_bytes")
        nc.sync.dma_start(
            d_bytes[:].bitcast(I32), d_scales[0].bitcast(I32).unsqueeze(1).to_broadcast([P // BLOCK, BLOCK, G // PACK])
        )
        x_table = new([P, T], I32, "x_table")
        nc.sync.dma_start(x_table[:], x_words[0].rearrange("p n t -> p (n t)").bitcast(I32))
        gs_sb = new([P, PACK], F32, "gs_sb")
        nc.sync.dma_start(gs_sb[:], gs.rearrange("(p t) o -> p (t o)", t=PACK))
        cand_sb = load_list(cand, "cand_sb")
        n1_sb = load_list(n1, "n1_sb")
        d_table = new([P, G], I32, "d_table")
        nc.sync.dma_start(d_table[:], d_words[0].rearrange("p n t -> p (n t)").bitcast(I32))
        n2_sb = load_list(n2, "n2_sb")
        n3_sb = load_list(n3, "n3_sb")
        n4_sb = load_list(n4, "n4_sb")

        gs_h = new([P, PACK], F32, "gs_h")
        nc.scalar.activation(gs_h[:], gs_sb[:], ACT.Copy, scale=SIXTEENTH)

        d_plane = new([P, H], U8, "d_plane")
        nc.gpsimd.memset(d_plane[:], 0)

        xq_plane = new([P, S], U8, "xq_plane")
        nc.vector.tensor_copy(xq_plane[:], x_bytes[:].indirect(offs_sb[:]))
        d_bytes_picked = new([P, H], U8, "d_bytes_picked")
        nc.vector.tensor_copy(d_bytes_picked[:], d_bytes[:].indirect(k1_sb[:]))
        d_bytes_dealt = new([P, H], U8, "d_bytes_dealt")
        nc.vector.tensor_copy(
            d_bytes_dealt[:].rearrange("p (t m) -> p t m", t=PACK), d_bytes_picked[:].rearrange("p (m t) -> p t m", t=PACK)
        )
        for q in range(P // QUADRANT):
            nc.scalar.dma_start(
                d_plane[QUADRANT * q : QUADRANT * q + PACK, :].bitcast(I32),
                d_bytes_dealt[QUADRANT * q : QUADRANT * (q + 1) : BLOCK, :].bitcast(I32),
            )
        xq_codes = new([P, S], U32, "xq_codes")
        nc.vector.tensor_copy(xq_codes[:], x_table[:].bitcast(U32).indirect(offs_sb[:]))
        d_picked = [new([P, H // 2], U32, "d_picked%d" % u) for u in range(2)]
        for u in range(2):
            picked = d_table[:].bitcast(U32).indirect(entries(k1_sb, u * H // 2, (u + 1) * H // 2))
            nc.vector.tensor_copy(d_picked[u][:], picked)
        d_codes = new([P, H], U32, "d_codes")
        lines = H // 2 // (PACK * LINE)
        for u in range(2):
            nc.vector.tensor_copy(
                d_codes[:].rearrange("p (t c i) -> p c t i", t=PACK, i=LINE)[:, lines * u : lines * (u + 1), :, :],
                d_picked[u][:].rearrange("p (c i t) -> p c t i", t=PACK, i=LINE),
            )

        h_ps = [psum.tile([P, S], F32, name="h_ps%d" % t) for t in range(PACK)]
        for t in range(PACK):
            cols = slice(P * t, P * (t + 1))
            nc.tensor.matmul_mx(
                h_ps[t][:],
                lhsT=d_codes[:, cols].bitcast(FP8X4),
                lhsT_scale=d_plane[:, cols],
                rhs=xq_codes[:].bitcast(FP8X4),
                rhs_scale=xq_plane[:],
                start=True,
                stop=True,
            )

        gs_zero = new([P, PACK], F32, "gs_zero")
        nc.gpsimd.tensor_scalar(gs_zero[:], gs_sb[:], 0.0, None, ALU.is_equal)
        gs_safe = new([P, PACK], F32, "gs_safe")
        nc.gpsimd.tensor_tensor(gs_safe[:], gs_sb[:], gs_zero[:], ALU.add)

        cand_bytes = new([P, C], U8, "cand_bytes", "d_table")
        nc.vector.tensor_copy(cand_bytes[:], x_bytes[:].indirect(cand_sb[:]))
        gs_inv = new([P, PACK], F32, "gs_inv", "d_picked1")
        nc.vector.reciprocal(gs_inv[:], gs_safe[:])
        cand_codes = new([P, C], U32, "cand_codes", "d_picked0")
        nc.vector.tensor_copy(
            cand_codes[:].rearrange("p (t b v) -> p b t v", t=PACK, v=BLOCK), x_table[:].bitcast(U32).indirect(cand_sb[:])
        )
        cand_plane = new([P, C], U8, "cand_plane")
        nc.vector.tensor_copy(
            cand_plane[:].bitcast(I32).rearrange("p (t b v) -> p b t v", t=PACK, v=BLOCK // PACK),
            cand_bytes[:].bitcast(I32).rearrange("p (b t v) -> p b t v", t=PACK, v=BLOCK // PACK),
        )

        st = [[new([P, HALF], F32, "st%d_%d" % (t, u)) for u in range(2)] for t in range(PACK)]
        th = [new([P, S], F32, "th%d" % t) for t in range(PACK)]
        z32_tags = ("z32_0", "d_picked1", "z32_0")
        z32 = {}
        z16 = {}
        s_ps = [psum.tile([P, S], F32, name="s_ps%d" % t) for t in range(PACK)]
        s_sb = [new([P, S], F32, "s_sb%d" % t) for t in range(PACK)]

        def make_st(t):
            window = new([P, S], F32, "h_window%d" % t)
            plain = new([P, S], F32, "h_plain%d" % t)
            nc.scalar.activation(window[:], h_ps[t][:], ACT.Copy, scale=gs_h[:, t : t + 1])
            nc.scalar.activation(plain[:], h_ps[t][:], ACT.Copy, scale=gs_h[:, t : t + 1])
            for u in range(2):
                a, b = u * HALF, (u + 1) * HALF
                nc.vector.tensor_tensor(st[t][u][:], window[:].indirect(entries(n1_sb, a, b)), plain[:, a:b], ALU.add)

        def make_tanh(t):
            for u in range(2):
                nc.scalar.activation(th[t][:, u * HALF : (u + 1) * HALF], st[t][u][:], ACT.Tanh, scale=gs_inv[:, t : t + 1])

        def make_z(t, c):
            a, b = CHUNKS[c]
            if t == 0:
                z32[c] = new([P, PACK, b - a], F32, "z32_%d" % c, z32_tags[c])
            u, a0 = divmod(a, HALF)
            picked = th[t][:].indirect(entries(n2_sb, a, b))
            nc.vector.tensor_tensor(z32[c][:, t, :], picked, st[t][u][:, a0 : a0 + b - a], ALU.mult)

        def round_z(c):
            a, b = CHUNKS[c]
            z16[c] = new([P, (b - a) * PACK], BF16, "z16_%d" % c)
            dst = z16[c][:].rearrange("p (n i t) -> p n t i", i=LINE, t=PACK)
            src = z32[c][:].rearrange("p t (n i) -> p n t i", i=LINE)
            if c == len(CHUNKS) - 1:
                nc.vector.tensor_copy(dst, src)
            else:
                nc.scalar.copy(dst, src)

        def score(c):
            a, b = CHUNKS[c]
            codes = new([P, b - a], U32, "z_codes%d" % c)
            plane = new([P, b - a], U8, "z_plane%d" % c)
            nc.vector.quantize_mx(codes[:].bitcast(FP8X4), plane[:], z16[c][:])
            for t in range(PACK):
                cols = slice(P * t, P * (t + 1))
                nc.tensor.matmul_mx(
                    s_ps[t][:, a:b],
                    lhsT=cand_codes[:, cols].bitcast(FP8X4),
                    lhsT_scale=cand_plane[:, cols],
                    rhs=codes[:].bitcast(FP8X4),
                    rhs_scale=plane[:],
                    start=True,
                    stop=True,
                )
                nc.scalar.activation(s_sb[t][:, a:b], s_ps[t][:, a:b], ACT.Copy, scale=SIXTEENTH)

        make_st(0)
        make_st(1)
        for t in range(PACK):
            make_tanh(t)
            if t > 0:
                make_z(t - 1, 0)
            if t + 2 < PACK:
                make_st(t + 2)
        make_z(PACK - 1, 0)
        round_z(0)
        for c in range(1, len(CHUNKS)):
            for t in range(PACK):
                make_z(t, c)
            score(c - 1)
            round_z(c)
        score(len(CHUNKS) - 1)

        out_rows = out.rearrange("(b t v) c -> t b v c", t=PACK, v=BLOCK)
        pa = [new([P, W], F32, "pa%d" % t) for t in range(PACK)]
        gap = [new([P, W], F32, "gap%d" % t) for t in range(PACK)]
        rise = [new([P, W], F32, "rise%d" % t) for t in range(PACK)]
        for first in range(0, PACK, 2):
            for t in (first, first + 1):
                nc.vector.tensor_copy(pa[t][:], s_sb[t][:].indirect(n3_sb[:]))
            for t in (first, first + 1):
                nc.vector.tensor_tensor(gap[t][:], s_sb[t][:].indirect(n4_sb[:]), pa[t][:], ALU.subtract)
                nc.scalar.activation(rise[t][:], gap[t][:], ACT.Relu)
        for t in range(PACK):
            nc.vector.tensor_tensor(s_sb[t][:].indirect(n3_sb[:]), pa[t][:], rise[t][:], ALU.add)
            nc.sync.dma_start(out_rows[t], s_sb[t][:])
